import numpy as np
import ml_dtypes


def mxq(x, axis, fmt="e4m3"):
    dtype, down = {"e4m3": (ml_dtypes.float8_e4m3fn, 7), "e5m2": (ml_dtypes.float8_e5m2, 14)}[fmt]
    v = np.moveaxis(np.asarray(x, np.float32).astype(ml_dtypes.bfloat16).astype(np.float64), axis, -1)
    blocks = v.reshape(v.shape[:-1] + (-1, 32))
    amax = np.abs(blocks).max(-1, keepdims=True)
    byte = np.maximum(np.where(amax > 0, np.frexp(amax)[1] - 1 + 127, 0) - down, 1)
    scale = np.exp2(byte - 127.0)
    codes = (blocks / scale).astype(np.float32).astype(dtype).astype(np.float64)
    return np.moveaxis((codes * scale).reshape(v.shape), -1, axis)


WIDE = False


def mx_kscale(k):
    if not WIDE:
        return np.ones(k)
    levels = np.array([10, -10, 5, -5, 0])
    if k % 512:
        return np.exp2(np.random.permutation(np.resize(levels, k // 32))).repeat(32)
    a = np.empty((k // 512, 16))
    for p in range(k // 512):
        a[p, :8] = np.random.permutation(np.resize(levels, 8))
        for g in range(8):
            far = levels[np.abs(levels - a[p, g]) >= 10]
            a[p, g + 8] = far[np.random.randint(len(far))]
    return np.exp2(a.ravel()).repeat(32)


BF16 = ml_dtypes.bfloat16


def bf(x):
    return np.asarray(x, np.float32).astype(BF16)


def f64(x):
    return np.asarray(x).astype(np.float64)


E2M1 = np.array([0.0, 0.5, 1.0, 1.5, 2.0, 3.0, 4.0, 6.0, -0.0, -0.5, -1.0, -1.5, -2.0, -3.0, -4.0, -6.0])


def pack_weight(w, fmt):
    k, n = w.shape
    w = f64(bf(w)).reshape(k // 32, 32, n)
    amax = np.abs(w).max(1)
    if fmt == "e4m3":
        byte = np.frexp(amax)[1] - 1 + 127 - 7
    else:
        mant, ex = np.frexp(amax / 6.0)
        byte = np.where(mant > 0.5, ex, ex - 1) + 127
    byte = np.clip(np.where(amax > 0, byte, 1), 1, 254)
    scaled = (w * np.exp2(127.0 - byte)[:, None, :]).reshape(k, n).astype(np.float32)
    by_word = np.ascontiguousarray(scaled.reshape(k // 512, 128, 4, n).transpose(0, 1, 3, 2))
    if fmt == "e4m3":
        words = by_word.astype(ml_dtypes.float8_e4m3fn).view(np.uint8)
    else:
        c = by_word.astype(ml_dtypes.float4_e2m1fn).view(np.uint8) & 0xF
        words = c[..., 0::2] | (c[..., 1::2] << 4)
    return np.ascontiguousarray(words), np.ascontiguousarray(byte.astype(np.uint8).reshape(k // 512, 16, n))


def unpack_weight(words, scales, fmt):
    g, p, n, _ = words.shape
    if fmt == "e4m3":
        vals = np.ascontiguousarray(words).view(ml_dtypes.float8_e4m3fn).astype(np.float64)
    else:
        nib = np.empty((g, p, n, 4), np.uint8)
        nib[..., 0::2] = words & 0xF
        nib[..., 1::2] = words >> 4
        vals = E2M1[nib]
    vals = vals * np.repeat(np.exp2(scales.astype(np.float64) - 127.0), 8, axis=1)[..., None]
    return vals.transpose(0, 1, 3, 2).reshape(g * 512, n)
def pack4(w):
    words, scales = pack_weight(w, "e2m1")
    return words.reshape(words.shape[0], 128, -1), scales


def unpack4(words, scales):
    return unpack_weight(words.reshape(words.shape[0], 128, -1, 2), scales, "e2m1")


def planes(Y):
    n, m = Y.shape
    b = f64(bf(Y)).reshape(n // 32, 32, m)
    amax = np.abs(b).max(1)
    byte = np.clip(np.where(amax > 0, np.frexp(amax)[1] - 1 + 127 - 7, 1), 1, 254)
    codes = (b * np.exp2(127.0 - byte)[:, None, :]).reshape(n, m).astype(np.float32).astype(ml_dtypes.float8_e4m3fn).view(np.uint8)
    words = codes.reshape(n // 512, 128, 4, m).transpose(0, 1, 3, 2)
    return np.ascontiguousarray(words), np.ascontiguousarray(byte.astype(np.uint8).reshape(n // 512, 16, m))


M, K, R, N = 1024, 1536, 1024, 2048
FP8 = "e4m3"

def setup_inputs():
    s = mx_kscale(K)
    t = mx_kscale(R)
    data = np.random.randn(K, M) / s[:, None]
    left = np.random.randn(K, R) / np.sqrt(K) * s[:, None] * t[None, :]
    right = np.random.randn(R, N) / np.sqrt(R) / t[:, None]
    b_words, b_scales = pack_weight(data, FP8)
    l_words, l_scales = pack4(left)
    return {
        "b_words": b_words,
        "b_scales": b_scales,
        "l_words": l_words,
        "l_scales": l_scales,
        "v": bf(right),
        "sigma": bf(0.3 + 1.7 * np.random.rand(R)),
        "alpha": bf(0.1 + 0.9 * np.random.rand(M)),
        "spread": bf(np.exp(0.8 * np.random.randn(N))),
        "mean": bf(0.5 * np.random.randn(N)),
    }

def reference(b_words, b_scales, l_words, l_scales, v, sigma, alpha, spread, mean):
    B = unpack_weight(b_words, b_scales, FP8)
    L = unpack4(l_words, l_scales)
    sg = f64(sigma)[:, None]
    C = L.T @ B
    H = C * sg / (sg * sg + f64(alpha)[None, :])
    Z = mxq(f64(v), 0, FP8).T @ mxq(H, 0, FP8)
    y = f64(mean)[:, None] + f64(spread)[:, None] * Z
    Y = y.reshape(N, M)
    words, scales = planes(Y)
    return y, words, scales

@@ -1,0 +1,407 @@
+from contextlib import ExitStack
+
+import concourse.mybir as mybir
+from concourse.masks import make_identity
+
+M, K, R, N = 1024, 1536, 1024, 2048
+FLOPS = 2 * K * R * M + 2 * R * N * M
+
+F32 = mybir.dt.float32
+BF16 = mybir.dt.bfloat16
+I32 = mybir.dt.int32
+U32 = mybir.dt.uint32
+U8 = mybir.dt.uint8
+FP8X4 = mybir.dt.float8_e4m3fn_x4
+FP4X4 = mybir.dt.float4_e2m1fn_x4
+ACT = mybir.ActivationFunctionType
+ALU = mybir.AluOpType
+AXIS = mybir.AxisListType
+
+P = 128
+PACK = 4
+BANK = 512
+K_PASSES = K // 512
+R_PASSES = R // 512
+HALVES = M // BANK
+GROUPS = N // 512
+
+
+def tile_damped_basis_estimate_h2_kernel(
+    tc, b_words, b_scales, l_words, l_scales, v, sigma, alpha, spread, mean, out_0, out_1, out_2
+):
+    nc = tc.nc
+    with ExitStack() as ctx:
+        keep = ctx.enter_context(tc.tile_pool(name="keep", bufs=1))
+        stage = ctx.enter_context(tc.tile_pool(name="stage", bufs=3))
+        psum = ctx.enter_context(tc.psum_pool(name="psum", bufs=1))
+        ctx.enter_context(tc.manual_schedule())
+
+        free_banks = [0, 1, 2, 3, 4, 5]
+
+        def bank(number):
+            return psum.tile([P, BANK], F32, name="bank%d" % number, tag="bank%d" % number)
+
+        l_raw = keep.tile([P, K_PASSES, 2 * R], U8, align_bytes=64)
+        l_codes = keep.tile([P, K_PASSES, 2 * R], U8, align_bytes=64)
+        ls_raw = keep.tile([P, K_PASSES, R], U8, align_bytes=64)
+        ls_plane = keep.tile([P, K_PASSES, R], U8, align_bytes=64)
+        bs_plane = keep.tile([P, K_PASSES, M], U8, align_bytes=64)
+        b_codes = {}
+        for h in range(HALVES):
+            for k in range(K_PASSES):
+                b_codes[h, k] = keep.tile([P, BANK], U32, align_bytes=64, name="b_codes%d%d" % (h, k))
+        v_raw = {}
+        for g in range(R_PASSES):
+            for x in range(GROUPS):
+                v_raw[g, x] = keep.tile([P, PACK, 512], BF16, align_bytes=64, name="v_raw%d%d" % (g, x))
+        v_codes, v_plane = {}, {}
+        for g in range(R_PASSES):
+            for x in range(GROUPS):
+                v_codes[g, x] = keep.tile([P, 512], U32, align_bytes=64, name="v_codes%d%d" % (g, x))
+                v_plane[g, x] = keep.tile([P, 512], U8, align_bytes=64, name="v_plane%d%d" % (g, x))
+        h_codes, h_plane = {}, {}
+        for g in range(R_PASSES):
+            for h in range(HALVES):
+                h_codes[g, h] = keep.tile([P, BANK], U32, align_bytes=64, name="h_codes%d%d" % (g, h))
+                h_plane[g, h] = keep.tile([P, BANK], U8, align_bytes=64, name="h_plane%d%d" % (g, h))
+        y_plane = keep.tile([P, GROUPS, M], U8, align_bytes=64)
+        ident = keep.tile([P, P], F32)
+        sigma_block = keep.tile([P, 8, 8], BF16)
+        alpha_col = keep.tile([P, HALVES, PACK], BF16)
+        spread_raw = keep.tile([P, GROUPS, PACK], BF16)
+        mean_raw = keep.tile([P, GROUPS, PACK], BF16)
+        spread_col = keep.tile([P, GROUPS, PACK], F32)
+        mean_col = keep.tile([P, GROUPS, PACK], F32)
+        own = keep.tile([P, 8], F32)
+        picked = keep.tile([P, 8, 8], F32)
+        sigma_col = keep.tile([P, 8], F32)
+        sigma_sq = keep.tile([P, 8], F32)
+        inv_sigma = keep.tile([P, 8], F32)
+        ln_sigma_sq = keep.tile([P, 8], F32)
+        ln_alpha = keep.tile([P, HALVES * PACK], F32)
+        one = keep.tile([P, 1], F32)
+        warm = keep.tile([P, 1], F32)
+
+        v_rows = v.rearrange("(b g t i) n -> g t b i n", g=R_PASSES, t=PACK, i=8)
+
+        def load_v(g, x):
+            for t in range(PACK):
+                nc.sync.dma_start(out=v_raw[g, x][:, t, :], in_=v_rows[g, t][:, :, 512 * x : 512 * (x + 1)])
+
+        def load_b(h, k):
+            words = b_words[k].rearrange("p n t -> p (n t)")[:, PACK * BANK * h : PACK * BANK * (h + 1)]
+            nc.sync.dma_start(out=b_codes[h, k][:].bitcast(I32), in_=words.bitcast(I32))
+
+        def load_scale_rows(plane, rows):
+            for q in range(4):
+                nc.sync.dma_start(
+                    out=plane[32 * q : 32 * q + 4, :, :].bitcast(I32),
+                    in_=rows[:, 4 * q : 4 * q + 4, :].rearrange("k r n -> r k n").bitcast(I32),
+                )
+
+        nc.vector.memset(ls_raw[:].bitcast(I32), 0)
+        nc.vector.memset(bs_plane[:].bitcast(I32), 0)
+        nc.vector.memset(one[:], 1.0)
+        nc.scalar.activation(out=warm[:], in_=one[:], func=ACT.Ln)
+        make_identity(nc, ident[:])
+
+        nc.sync.dma_start(
+            out=sigma_block[:].rearrange("p c i -> p (c i)"),
+            in_=sigma.rearrange("(b w) -> b w", w=64).unsqueeze(1).to_broadcast([16, 8, 64]),
+        )
+        nc.sync.dma_start(out=alpha_col[:], in_=alpha.rearrange("(h p m) -> p h m", h=HALVES, m=PACK))
+        load_v(0, 0)
+        nc.sync.dma_start(out=l_raw[:].bitcast(I32), in_=l_words.rearrange("k p n -> p k n").bitcast(I32))
+        load_scale_rows(ls_raw, l_scales)
+        load_b(0, 0)
+        load_scale_rows(bs_plane, b_scales)
+        load_v(1, 0)
+        load_b(0, 1)
+        load_b(0, 2)
+        nc.sync.dma_start(out=spread_raw[:], in_=spread.rearrange("(x p t) -> p x t", x=GROUPS, t=PACK))
+        nc.sync.dma_start(out=mean_raw[:], in_=mean.rearrange("(x p t) -> p x t", x=GROUPS, t=PACK))
+        load_v(0, 1)
+        load_b(1, 0)
+        load_b(1, 1)
+        load_v(0, 2)
+        load_b(1, 2)
+        load_v(1, 1)
+        load_v(1, 2)
+        load_v(1, 3)
+        load_v(0, 3)
+
+        nc.vector.tensor_reduce(
+            out=own[:], in_=ident[:].rearrange("p (b i) -> p i b", i=8), axis=AXIS.X, op=ALU.add
+        )
+        nc.scalar.activation(out=ln_alpha[:], in_=alpha_col[:].rearrange("p h m -> p (h m)"), func=ACT.Ln)
+        nc.vector.tensor_tensor(
+            out=picked[:], in0=sigma_block[:], in1=own[:].unsqueeze(1).to_broadcast([P, 8, 8]), op=ALU.mult
+        )
+        nc.vector.tensor_reduce(out=sigma_col[:], in_=picked[:], axis=AXIS.X, op=ALU.add)
+        nc.vector.tensor_tensor(out=sigma_sq[:], in0=sigma_col[:], in1=sigma_col[:], op=ALU.mult)
+        nc.vector.reciprocal(out=inv_sigma[:], in_=sigma_col[:])
+        nc.scalar.activation(out=ln_sigma_sq[:], in_=sigma_sq[:], func=ACT.Ln)
+
+        ln_alpha_row = {}
+        for h in range(HALVES):
+            ln_alpha_row[h] = bank(6 + h)
+            for m in range(PACK):
+                col = PACK * h + m
+                nc.tensor.transpose(
+                    ln_alpha_row[h][:, P * m : P * (m + 1)],
+                    ln_alpha[:, col : col + 1].to_broadcast([P, P]),
+                    ident[:],
+                )
+
+        def order_l(k):
+            nc.vector.tensor_copy(
+                out=l_codes[:, k, :].bitcast(I32).rearrange("p (c b w) -> p c b w", c=8, w=4),
+                in_=l_raw[:, k, :].bitcast(I32).rearrange("p (b c w) -> p c b w", c=8, w=4),
+            )
+            nc.vector.tensor_copy(
+                out=ls_plane[:, k, :].bitcast(I32).rearrange("p (c b w) -> p c b w", c=8, w=2),
+                in_=ls_raw[:, k, :].bitcast(I32).rearrange("p (b c w) -> p c b w", c=8, w=2),
+            )
+
+        c_number, z_number = {}, {}
+        c_bank, gate, h_rows, h_packed, v_packed, z_bank, y_rows, y_packed = {}, {}, {}, {}, {}, {}, {}, {}
+
+        def copy_on(engine, out, in_):
+            if engine == "scalar":
+                nc.scalar.copy(out=out, in_=in_)
+            else:
+                nc.vector.tensor_copy(out=out, in_=in_)
+
+        def analyse(g, h, u):
+            for t in (2 * u, 2 * u + 1):
+                c = PACK * g + t
+                c_number[g, h, t] = free_banks.pop(0)
+                c_bank[g, h, t] = bank(c_number[g, h, t])
+                for k in range(K_PASSES):
+                    nc.tensor.matmul_mx(
+                        out=c_bank[g, h, t][:],
+                        lhsT=l_codes[:, k, 2 * P * c : 2 * P * (c + 1)].bitcast(FP4X4),
+                        lhsT_scale=ls_plane[:, k, P * c : P * (c + 1)],
+                        rhs=b_codes[h, k][:].bitcast(FP8X4),
+                        rhs_scale=bs_plane[:, k, BANK * h : BANK * (h + 1)],
+                        start=(k == 0),
+                        stop=(k == K_PASSES - 1),
+                    )
+
+        def gates(g, h):
+            for t in range(PACK):
+                c = PACK * g + t
+                gate[g, h, t] = stage.tile([P, BANK], F32, name="gate", tag="gate", bufs=16)
+                nc.scalar.activation(
+                    out=gate[g, h, t][:].rearrange("p (k m) -> p k m", m=PACK),
+                    in_=ln_alpha_row[h][:].rearrange("p (m k) -> p k m", m=PACK),
+                    func=ACT.Sigmoid,
+                    scale=-1.0,
+                    bias=ln_sigma_sq[:, c : c + 1],
+                )
+            if (1 - g, h, 0) in gate:
+                free_banks.append(6 + h)
+
+        def damp(g, h, u):
+            if u == 0:
+                h_rows[g, h] = stage.tile([P, PACK, BANK], BF16, name="h_rows", tag="h_rows", bufs=3)
+            for t in (2 * u, 2 * u + 1):
+                c = PACK * g + t
+                nc.vector.scalar_tensor_tensor(
+                    out=h_rows[g, h][:, t, :],
+                    in0=c_bank[g, h, t][:],
+                    scalar=inv_sigma[:, c : c + 1],
+                    in1=gate[g, h, t][:],
+                    op0=ALU.mult,
+                    op1=ALU.mult,
+                )
+                free_banks.append(c_number[g, h, t])
+
+        def interleave(engine, rows):
+            packed = stage.tile([P, BANK, PACK], BF16, align_bytes=64, name="packed", tag="packed", bufs=7)
+            copy_on(
+                engine,
+                packed[:].rearrange("p (c i) t -> p c t i", i=4),
+                rows[:].rearrange("p t (c i) -> p c t i", i=4),
+            )
+            return packed
+
+        def quantise(codes, plane, packed):
+            nc.vector.quantize_mx(
+                out=codes.bitcast(FP8X4), scales=plane, in_=packed[:].rearrange("p n t -> p (n t)")
+            )
+
+        def pack_h(engine, g, h):
+            h_packed[g, h] = interleave(engine, h_rows[g, h])
+
+        def quant_h(g, h):
+            quantise(h_codes[g, h][:], h_plane[g, h][:], h_packed[g, h])
+
+        def pack_v(engine, g, x):
+            packed = stage.tile([P, BANK, PACK], BF16, align_bytes=64, name="packed", tag="packed", bufs=7)
+            copy_on(
+                engine,
+                packed[:].rearrange("p (s m) t -> p m t s", s=PACK),
+                v_raw[g, x][:].rearrange("p t (m s) -> p m t s", s=PACK),
+            )
+            v_packed[g, x] = packed
+
+        def quant_v(g, x):
+            quantise(v_codes[g, x][:], v_plane[g, x][:], v_packed[g, x])
+
+        def synthesise(x, h, u):
+            for s in (2 * u, 2 * u + 1):
+                z_number[x, h, s] = free_banks.pop(0)
+                z_bank[x, h, s] = bank(z_number[x, h, s])
+                for g in range(R_PASSES):
+                    nc.tensor.matmul_mx(
+                        out=z_bank[x, h, s][:],
+                        lhsT=v_codes[g, x][:, P * s : P * (s + 1)].bitcast(FP8X4),
+                        lhsT_scale=v_plane[g, x][:, P * s : P * (s + 1)],
+                        rhs=h_codes[g, h][:].bitcast(FP8X4),
+                        rhs_scale=h_plane[g, h][:],
+                        start=(g == 0),
+                        stop=(g == R_PASSES - 1),
+                    )
+
+        def finish_y(engine, x, h, u):
+            if u == 0:
+                y_rows[x, h] = stage.tile([P, PACK, BANK], F32, name="y_rows", tag="y_rows", bufs=6)
+            target = out_0[512 * x : 512 * (x + 1), BANK * h : BANK * (h + 1)].rearrange("(p s) m -> p s m", s=PACK)
+            for s in (2 * u, 2 * u + 1):
+                if engine == "scalar":
+                    nc.scalar.activation(
+                        out=y_rows[x, h][:, s, :],
+                        in_=z_bank[x, h, s][:],
+                        func=ACT.Identity,
+                        scale=spread_col[:, x, s : s + 1],
+                        bias=mean_col[:, x, s : s + 1],
+                    )
+                else:
+                    nc.vector.tensor_scalar(
+                        out=y_rows[x, h][:, s, :],
+                        in0=z_bank[x, h, s][:],
+                        scalar1=spread_col[:, x, s : s + 1],
+                        scalar2=mean_col[:, x, s : s + 1],
+                        op0=ALU.mult,
+                        op1=ALU.add,
+                    )
+                free_banks.append(z_number[x, h, s])
+            rows = slice(2 * u, 2 * u + 2)
+            nc.sync.dma_start(out=target[:, rows, :], in_=y_rows[x, h][:, rows, :])
+
+        def pack_y(engine, x, h):
+            y_packed[x, h] = interleave(engine, y_rows[x, h])
+
+        def quant_y(x, h):
+            y_codes = stage.tile([P, BANK], U32, align_bytes=64, name="y_codes", tag="y_codes", bufs=5)
+            quantise(y_codes[:], y_plane[:, x, BANK * h : BANK * (h + 1)], y_packed[x, h])
+            words = out_1[x].rearrange("p m t -> p (m t)")[:, PACK * BANK * h : PACK * BANK * (h + 1)]
+            nc.sync.dma_start(out=words.bitcast(I32), in_=y_codes[:].bitcast(I32))
+
+        def store_scale_rows(queue, lo, hi):
+            for q in range(4):
+                queue.dma_start(
+                    out=out_2[lo:hi, 4 * q : 4 * q + 4, :].rearrange("x r m -> r x m").bitcast(I32),
+                    in_=y_plane[32 * q : 32 * q + 4, lo:hi, :].bitcast(I32),
+                )
+
+        pack_v("vector", 0, 0)
+        order_l(0)
+        gates(0, 0)
+        order_l(1)
+        quant_v(0, 0)
+        order_l(2)
+        pack_v("vector", 1, 0)
+        gates(1, 0)
+        analyse(0, 0, 0)
+        nc.vector.tensor_copy(out=spread_col[:], in_=spread_raw[:])
+        nc.vector.tensor_copy(out=mean_col[:], in_=mean_raw[:])
+        analyse(0, 0, 1)
+        quant_v(1, 0)
+        gates(0, 1)
+        damp(0, 0, 0)
+        gates(1, 1)
+        pack_v("vector", 0, 1)
+        analyse(1, 0, 0)
+        damp(0, 0, 1)
+        damp(1, 0, 0)
+        pack_v("scalar", 0, 2)
+        quant_v(0, 1)
+        analyse(1, 0, 1)
+        damp(1, 0, 1)
+        analyse(0, 1, 0)
+        analyse(0, 1, 1)
+        analyse(1, 1, 0)
+        pack_v("vector", 1, 1)
+        quant_v(0, 2)
+        pack_h("scalar", 0, 0)
+        damp(0, 1, 0)
+        quant_h(0, 0)
+        pack_h("scalar", 1, 0)
+        damp(0, 1, 1)
+        quant_h(1, 0)
+        analyse(1, 1, 1)
+        damp(1, 1, 0)
+        synthesise(0, 0, 0)
+        quant_v(1, 1)
+        pack_h("vector", 0, 1)
+        synthesise(0, 0, 1)
+        pack_v("scalar", 1, 2)
+        damp(1, 1, 1)
+        finish_y("scalar", 0, 0, 0)
+        synthesise(1, 0, 0)
+        synthesise(1, 0, 1)
+        finish_y("scalar", 0, 0, 1)
+        quant_v(1, 2)
+        finish_y("scalar", 1, 0, 0)
+        pack_h("vector", 1, 1)
+        finish_y("scalar", 1, 0, 1)
+        quant_h(0, 1)
+        synthesise(2, 0, 0)
+        quant_h(1, 1)
+        pack_y("vector", 0, 0)
+        synthesise(2, 0, 1)
+        synthesise(0, 1, 0)
+        finish_y("scalar", 2, 0, 0)
+        finish_y("scalar", 2, 0, 1)
+        synthesise(1, 1, 0)
+        synthesise(2, 1, 0)
+        finish_y("scalar", 0, 1, 0)
+        finish_y("scalar", 1, 1, 0)
+        synthesise(0, 1, 1)
+        synthesise(1, 1, 1)
+        pack_v("vector", 0, 3)
+        quant_y(0, 0)
+        pack_v("vector", 1, 3)
+        finish_y("scalar", 2, 1, 0)
+        finish_y("scalar", 0, 1, 1)
+        quant_v(0, 3)
+        quant_v(1, 3)
+        synthesise(2, 1, 1)
+        synthesise(3, 0, 0)
+        pack_y("vector", 1, 0)
+        synthesise(3, 0, 1)
+        finish_y("scalar", 1, 1, 1)
+        synthesise(3, 1, 0)
+        finish_y("scalar", 2, 1, 1)
+        finish_y("scalar", 3, 0, 0)
+        pack_y("vector", 2, 0)
+        finish_y("scalar", 3, 0, 1)
+        quant_y(1, 0)
+        pack_y("vector", 0, 1)
+        synthesise(3, 1, 1)
+        finish_y("scalar", 3, 1, 0)
+        finish_y("scalar", 3, 1, 1)
+        pack_y("vector", 2, 1)
+        quant_y(0, 1)
+        pack_y("scalar", 3, 1)
+        quant_y(2, 1)
+        pack_y("vector", 1, 1)
+        quant_y(2, 0)
+        quant_y(1, 1)
+        pack_y("vector", 3, 0)
+        store_scale_rows(nc.sync, 0, 3)
+        quant_y(3, 1)
+        quant_y(3, 0)
+        store_scale_rows(nc.scalar, 3, 4)

@@ -24,6 +24,9 @@ K_PASSES = K // 512
 R_PASSES = R // 512
 HALVES = M // BANK
 GROUPS = N // 512
+SPLIT_Y = (0, 1,)
+SPLIT_WORDS = (0, 1, 2, 3,)
+V_CHUNKS = {0: (0, 1), 1: (1, 2), 2: (2, 4)}
 
 
 def tile_damped_basis_estimate_h2_kernel(
@@ -36,15 +39,17 @@ def tile_damped_basis_estimate_h2_kernel(
         psum = ctx.enter_context(tc.psum_pool(name="psum", bufs=1))
         ctx.enter_context(tc.manual_schedule())
 
-        free_banks = [0, 1, 2, 3, 4, 5]
+        free_banks = [1, 2, 3, 4, 5, 0]
 
         def bank(number):
             return psum.tile([P, BANK], F32, name="bank%d" % number, tag="bank%d" % number)
 
-        l_raw = keep.tile([P, K_PASSES, 2 * R], U8, align_bytes=64)
-        l_codes = keep.tile([P, K_PASSES, 2 * R], U8, align_bytes=64)
+        l_raw, l_codes, ls_plane = {}, {}, {}
+        for g in range(R_PASSES):
+            l_raw[g] = keep.tile([P, K_PASSES, 1024], U8, align_bytes=64, name="l_raw%d" % g)
+            l_codes[g] = keep.tile([P, K_PASSES, 1024], U8, align_bytes=64, name="l_codes%d" % g)
+            ls_plane[g] = keep.tile([P, K_PASSES, 512], U8, align_bytes=64, name="ls_plane%d" % g)
         ls_raw = keep.tile([P, K_PASSES, R], U8, align_bytes=64)
-        ls_plane = keep.tile([P, K_PASSES, R], U8, align_bytes=64)
         bs_plane = keep.tile([P, K_PASSES, M], U8, align_bytes=64)
         b_codes = {}
         for h in range(HALVES):
@@ -52,8 +57,8 @@ def tile_damped_basis_estimate_h2_kernel(
                 b_codes[h, k] = keep.tile([P, BANK], U32, align_bytes=64, name="b_codes%d%d" % (h, k))
         v_raw = {}
         for g in range(R_PASSES):
-            for x in range(GROUPS):
-                v_raw[g, x] = keep.tile([P, PACK, 512], BF16, align_bytes=64, name="v_raw%d%d" % (g, x))
+            for lo, hi in V_CHUNKS.values():
+                v_raw[g, lo] = keep.tile([P, PACK, 512 * (hi - lo)], BF16, align_bytes=64, name="v_raw%d%d" % (g, lo))
         v_codes, v_plane = {}, {}
         for g in range(R_PASSES):
             for x in range(GROUPS):
@@ -64,14 +69,12 @@ def tile_damped_basis_estimate_h2_kernel(
             for h in range(HALVES):
                 h_codes[g, h] = keep.tile([P, BANK], U32, align_bytes=64, name="h_codes%d%d" % (g, h))
                 h_plane[g, h] = keep.tile([P, BANK], U8, align_bytes=64, name="h_plane%d%d" % (g, h))
-        y_plane = keep.tile([P, GROUPS, M], U8, align_bytes=64)
+        y_plane = keep.tile([P, M], U8, align_bytes=64)
         ident = keep.tile([P, P], F32)
         sigma_block = keep.tile([P, 8, 8], BF16)
-        alpha_col = keep.tile([P, HALVES, PACK], BF16)
-        spread_raw = keep.tile([P, GROUPS, PACK], BF16)
-        mean_raw = keep.tile([P, GROUPS, PACK], BF16)
-        spread_col = keep.tile([P, GROUPS, PACK], F32)
-        mean_col = keep.tile([P, GROUPS, PACK], F32)
+        vec_rows = keep.tile([P, 512], BF16)
+        ident_bf = keep.tile([P, P], BF16)
+        affine = keep.tile([P, 2 * GROUPS, PACK], F32)
         own = keep.tile([P, 8], F32)
         picked = keep.tile([P, 8, 8], F32)
         sigma_col = keep.tile([P, 8], F32)
@@ -82,11 +85,28 @@ def tile_damped_basis_estimate_h2_kernel(
         one = keep.tile([P, 1], F32)
         warm = keep.tile([P, 1], F32)
 
-        v_rows = v.rearrange("(b g t i) n -> g t b i n", g=R_PASSES, t=PACK, i=8)
+        v_rows = v.rearrange("(g b t i) n -> g t b i n", g=R_PASSES, t=PACK, i=8)
 
-        def load_v(g, x):
+        def load_v(g, chunk):
+            lo, hi = V_CHUNKS[chunk]
             for t in range(PACK):
-                nc.sync.dma_start(out=v_raw[g, x][:, t, :], in_=v_rows[g, t][:, :, 512 * x : 512 * (x + 1)])
+                nc.sync.dma_start(out=v_raw[g, lo][:, t, :], in_=v_rows[g, t][:, :, 512 * lo : 512 * hi])
+
+        def load_l(g):
+            words = l_words.rearrange("k p n -> p k n")[:, :, 1024 * g : 1024 * (g + 1)]
+            nc.sync.dma_start(out=l_raw[g][:].bitcast(I32), in_=words.bitcast(I32))
+
+        def load_sigma():
+            for g in range(R_PASSES):
+                blocks = sigma[512 * g : 512 * (g + 1)].rearrange("(b w) -> b w", w=32)
+                nc.sync.dma_start(
+                    out=sigma_block[:, PACK * g : PACK * (g + 1), :].rearrange("p c i -> p (c i)"),
+                    in_=blocks.unsqueeze(1).to_broadcast([16, 8, 32]),
+                )
+
+        def load_rows(first, vector):
+            rows = vector.rearrange("(a n) -> a n", n=512)
+            nc.sync.dma_start(out=vec_rows[first : first + rows.shape[0], :], in_=rows)
 
         def load_b(h, k):
             words = b_words[k].rearrange("p n t -> p (n t)")[:, PACK * BANK * h : PACK * BANK * (h + 1)]
@@ -103,37 +123,42 @@ def tile_damped_basis_estimate_h2_kernel(
         nc.vector.memset(bs_plane[:].bitcast(I32), 0)
         nc.vector.memset(one[:], 1.0)
         nc.scalar.activation(out=warm[:], in_=one[:], func=ACT.Ln)
+        nc.gpsimd.memset(vec_rows[:], 0.0)
+        make_identity(nc, ident_bf[:])
         make_identity(nc, ident[:])
 
-        nc.sync.dma_start(
-            out=sigma_block[:].rearrange("p c i -> p (c i)"),
-            in_=sigma.rearrange("(b w) -> b w", w=64).unsqueeze(1).to_broadcast([16, 8, 64]),
-        )
-        nc.sync.dma_start(out=alpha_col[:], in_=alpha.rearrange("(h p m) -> p h m", h=HALVES, m=PACK))
-        load_v(0, 0)
-        nc.sync.dma_start(out=l_raw[:].bitcast(I32), in_=l_words.rearrange("k p n -> p k n").bitcast(I32))
-        load_scale_rows(ls_raw, l_scales)
         load_b(0, 0)
+        load_sigma()
+        load_rows(8, alpha)
+        load_rows(0, spread)
+        load_rows(4, mean)
+        load_l(0)
+        load_scale_rows(ls_raw, l_scales)
         load_scale_rows(bs_plane, b_scales)
-        load_v(1, 0)
         load_b(0, 1)
         load_b(0, 2)
-        nc.sync.dma_start(out=spread_raw[:], in_=spread.rearrange("(x p t) -> p x t", x=GROUPS, t=PACK))
-        nc.sync.dma_start(out=mean_raw[:], in_=mean.rearrange("(x p t) -> p x t", x=GROUPS, t=PACK))
-        load_v(0, 1)
+        load_l(1)
+        load_v(1, 0)
         load_b(1, 0)
+        load_v(0, 0)
         load_b(1, 1)
-        load_v(0, 2)
+        load_v(0, 1)
         load_b(1, 2)
         load_v(1, 1)
+        load_v(0, 2)
         load_v(1, 2)
-        load_v(1, 3)
-        load_v(0, 3)
 
         nc.vector.tensor_reduce(
             out=own[:], in_=ident[:].rearrange("p (b i) -> p i b", i=8), axis=AXIS.X, op=ALU.add
         )
-        nc.scalar.activation(out=ln_alpha[:], in_=alpha_col[:].rearrange("p h m -> p (h m)"), func=ACT.Ln)
+        vec_cols = psum.tile([P, PACK, P], BF16, name="bank0", tag="bank0")
+        for t in range(PACK):
+            nc.tensor.transpose(vec_cols[:, t, :], vec_rows[:, t : 512 : PACK], ident_bf[:])
+        nc.scalar.activation(
+            out=ln_alpha[:].rearrange("p (h m) -> p h m", m=PACK),
+            in_=vec_cols[:, :, 8:10].rearrange("p m h -> p h m"),
+            func=ACT.Ln,
+        )
         nc.vector.tensor_tensor(
             out=picked[:], in0=sigma_block[:], in1=own[:].unsqueeze(1).to_broadcast([P, 8, 8]), op=ALU.mult
         )
@@ -153,35 +178,36 @@ def tile_damped_basis_estimate_h2_kernel(
                     ident[:],
                 )
 
-        def order_l(k):
+        def order_l(g):
             nc.vector.tensor_copy(
-                out=l_codes[:, k, :].bitcast(I32).rearrange("p (c b w) -> p c b w", c=8, w=4),
-                in_=l_raw[:, k, :].bitcast(I32).rearrange("p (b c w) -> p c b w", c=8, w=4),
+                out=l_codes[g][:].bitcast(I32).rearrange("p k (t b w) -> p t k b w", t=PACK, w=4),
+                in_=l_raw[g][:].bitcast(I32).rearrange("p k (b t w) -> p t k b w", t=PACK, w=4),
             )
             nc.vector.tensor_copy(
-                out=ls_plane[:, k, :].bitcast(I32).rearrange("p (c b w) -> p c b w", c=8, w=2),
-                in_=ls_raw[:, k, :].bitcast(I32).rearrange("p (b c w) -> p c b w", c=8, w=2),
+                out=ls_plane[g][:].bitcast(I32).rearrange("p k (t b w) -> p t k b w", t=PACK, w=2),
+                in_=ls_raw[:, :, 512 * g : 512 * (g + 1)].bitcast(I32).rearrange("p k (b t w) -> p t k b w", t=PACK, w=2),
             )
 
-        c_number, z_number = {}, {}
+        c_number, z_number, y_codes, y_done = {}, {}, {}, set()
         c_bank, gate, h_rows, h_packed, v_packed, z_bank, y_rows, y_packed = {}, {}, {}, {}, {}, {}, {}, {}
 
         def copy_on(engine, out, in_):
             if engine == "scalar":
                 nc.scalar.copy(out=out, in_=in_)
+            elif engine == "gpsimd":
+                nc.gpsimd.tensor_scalar(out=out, in0=in_, scalar1=1.0, scalar2=1.0, op0=ALU.mult, op1=ALU.mult)
             else:
                 nc.vector.tensor_copy(out=out, in_=in_)
 
         def analyse(g, h, u):
             for t in (2 * u, 2 * u + 1):
-                c = PACK * g + t
                 c_number[g, h, t] = free_banks.pop(0)
                 c_bank[g, h, t] = bank(c_number[g, h, t])
                 for k in range(K_PASSES):
                     nc.tensor.matmul_mx(
                         out=c_bank[g, h, t][:],
-                        lhsT=l_codes[:, k, 2 * P * c : 2 * P * (c + 1)].bitcast(FP4X4),
-                        lhsT_scale=ls_plane[:, k, P * c : P * (c + 1)],
+                        lhsT=l_codes[g][:, k, 2 * P * t : 2 * P * (t + 1)].bitcast(FP4X4),
+                        lhsT_scale=ls_plane[g][:, k, P * t : P * (t + 1)],
                         rhs=b_codes[h, k][:].bitcast(FP8X4),
                         rhs_scale=bs_plane[:, k, BANK * h : BANK * (h + 1)],
                         start=(k == 0),
@@ -222,7 +248,7 @@ def tile_damped_basis_estimate_h2_kernel(
             copy_on(
                 engine,
                 packed[:].rearrange("p (c i) t -> p c t i", i=4),
-                rows[:].rearrange("p t (c i) -> p c t i", i=4),
+                rows.rearrange("p t (c i) -> p c t i", i=4),
             )
             return packed
 
@@ -232,7 +258,7 @@ def tile_damped_basis_estimate_h2_kernel(
             )
 
         def pack_h(engine, g, h):
-            h_packed[g, h] = interleave(engine, h_rows[g, h])
+            h_packed[g, h] = interleave(engine, h_rows[g, h][:])
 
         def quant_h(g, h):
             quantise(h_codes[g, h][:], h_plane[g, h][:], h_packed[g, h])
@@ -242,7 +268,7 @@ def tile_damped_basis_estimate_h2_kernel(
             copy_on(
                 engine,
                 packed[:].rearrange("p (s m) t -> p m t s", s=PACK),
-                v_raw[g, x][:].rearrange("p t (m s) -> p m t s", s=PACK),
+                v_raw[g, min(x, 2)][:, :, 512 * max(x - 2, 0) : 512 * (max(x - 2, 0) + 1)].rearrange("p t (m s) -> p m t s", s=PACK),
             )
             v_packed[g, x] = packed
 
@@ -265,143 +291,152 @@ def tile_damped_basis_estimate_h2_kernel(
                     )
 
         def finish_y(engine, x, h, u):
-            if u == 0:
-                y_rows[x, h] = stage.tile([P, PACK, BANK], F32, name="y_rows", tag="y_rows", bufs=6)
-            target = out_0[512 * x : 512 * (x + 1), BANK * h : BANK * (h + 1)].rearrange("(p s) m -> p s m", s=PACK)
+            if x not in y_rows:
+                y_rows[x] = stage.tile([P, PACK, M], F32, name="y_rows", tag="y_rows", bufs=3)
+            target = out_0[512 * x : 512 * (x + 1), :].rearrange("(p s) m -> p s m", s=PACK)
+            cols = slice(BANK * h, BANK * (h + 1))
+            whole = (x, 1 - h, u) in y_done
+            y_done.add((x, h, u))
             for s in (2 * u, 2 * u + 1):
                 if engine == "scalar":
                     nc.scalar.activation(
-                        out=y_rows[x, h][:, s, :],
+                        out=y_rows[x][:, s, cols],
                         in_=z_bank[x, h, s][:],
                         func=ACT.Identity,
-                        scale=spread_col[:, x, s : s + 1],
-                        bias=mean_col[:, x, s : s + 1],
+                        scale=affine[:, x, s : s + 1],
+                        bias=affine[:, GROUPS + x, s : s + 1],
                     )
                 else:
                     nc.vector.tensor_scalar(
-                        out=y_rows[x, h][:, s, :],
+                        out=y_rows[x][:, s, cols],
                         in0=z_bank[x, h, s][:],
-                        scalar1=spread_col[:, x, s : s + 1],
-                        scalar2=mean_col[:, x, s : s + 1],
+                        scalar1=affine[:, x, s : s + 1],
+                        scalar2=affine[:, GROUPS + x, s : s + 1],
                         op0=ALU.mult,
                         op1=ALU.add,
                     )
                 free_banks.append(z_number[x, h, s])
+                if whole and x not in SPLIT_Y:
+                    nc.sync.dma_start(out=target[:, s, :], in_=y_rows[x][:, s, :])
             rows = slice(2 * u, 2 * u + 2)
-            nc.sync.dma_start(out=target[:, rows, :], in_=y_rows[x, h][:, rows, :])
+            if x in SPLIT_Y:
+                nc.sync.dma_start(out=target[:, rows, cols], in_=y_rows[x][:, rows, cols])
 
         def pack_y(engine, x, h):
-            y_packed[x, h] = interleave(engine, y_rows[x, h])
+            y_packed[x, h] = interleave(engine, y_rows[x][:, :, BANK * h : BANK * (h + 1)])
 
         def quant_y(x, h):
-            y_codes = stage.tile([P, BANK], U32, align_bytes=64, name="y_codes", tag="y_codes", bufs=5)
-            quantise(y_codes[:], y_plane[:, x, BANK * h : BANK * (h + 1)], y_packed[x, h])
-            words = out_1[x].rearrange("p m t -> p (m t)")[:, PACK * BANK * h : PACK * BANK * (h + 1)]
-            nc.sync.dma_start(out=words.bitcast(I32), in_=y_codes[:].bitcast(I32))
+            whole = x in y_codes
+            if not whole:
+                y_codes[x] = stage.tile([P, M], U32, align_bytes=64, name="y_codes", tag="y_codes", bufs=3)
+            cols = slice(BANK * h, BANK * (h + 1))
+            quantise(y_codes[x][:, cols], y_plane[4 * x :, cols], y_packed[x, h])
+            words = out_1[x].rearrange("p m t -> p (m t)").bitcast(I32)
+            if x in SPLIT_WORDS:
+                nc.sync.dma_start(out=words[:, cols], in_=y_codes[x][:, cols].bitcast(I32))
+            elif whole:
+                nc.sync.dma_start(out=words, in_=y_codes[x][:].bitcast(I32))
 
-        def store_scale_rows(queue, lo, hi):
+        def store_scale_rows():
             for q in range(4):
-                queue.dma_start(
-                    out=out_2[lo:hi, 4 * q : 4 * q + 4, :].rearrange("x r m -> r x m").bitcast(I32),
-                    in_=y_plane[32 * q : 32 * q + 4, lo:hi, :].bitcast(I32),
+                nc.scalar.dma_start(
+                    out=out_2[:, 4 * q : 4 * q + 4, :].bitcast(I32),
+                    in_=y_plane[32 * q : 32 * q + 16, :].bitcast(I32),
                 )
 
-        pack_v("vector", 0, 0)
-        order_l(0)
         gates(0, 0)
-        order_l(1)
-        quant_v(0, 0)
-        order_l(2)
-        pack_v("vector", 1, 0)
-        gates(1, 0)
+        order_l(0)
+        nc.vector.tensor_copy(out=affine[:], in_=vec_cols[:, :, 0 : 2 * GROUPS].rearrange("p t a -> p a t"))
         analyse(0, 0, 0)
-        nc.vector.tensor_copy(out=spread_col[:], in_=spread_raw[:])
-        nc.vector.tensor_copy(out=mean_col[:], in_=mean_raw[:])
-        analyse(0, 0, 1)
-        quant_v(1, 0)
-        gates(0, 1)
+        order_l(1)
+        gates(1, 0)
         damp(0, 0, 0)
-        gates(1, 1)
-        pack_v("vector", 0, 1)
+        analyse(0, 0, 1)
+        gates(0, 1)
         analyse(1, 0, 0)
+        pack_v("scalar", 0, 0)
+        pack_v("vector", 1, 0)
+        analyse(1, 0, 1)
         damp(0, 0, 1)
         damp(1, 0, 0)
-        pack_v("scalar", 0, 2)
-        quant_v(0, 1)
-        analyse(1, 0, 1)
-        damp(1, 0, 1)
         analyse(0, 1, 0)
+        quant_v(1, 0)
+        damp(1, 0, 1)
         analyse(0, 1, 1)
         analyse(1, 1, 0)
-        pack_v("vector", 1, 1)
-        quant_v(0, 2)
-        pack_h("scalar", 0, 0)
+        pack_h("vector", 0, 0)
         damp(0, 1, 0)
-        quant_h(0, 0)
-        pack_h("scalar", 1, 0)
         damp(0, 1, 1)
-        quant_h(1, 0)
+        quant_h(0, 0)
+        gates(1, 1)
+        pack_h("scalar", 1, 0)
+        quant_v(0, 0)
+        pack_h("scalar", 0, 1)
         analyse(1, 1, 1)
         damp(1, 1, 0)
-        synthesise(0, 0, 0)
-        quant_v(1, 1)
-        pack_h("vector", 0, 1)
-        synthesise(0, 0, 1)
-        pack_v("scalar", 1, 2)
         damp(1, 1, 1)
-        finish_y("scalar", 0, 0, 0)
-        synthesise(1, 0, 0)
-        synthesise(1, 0, 1)
-        finish_y("scalar", 0, 0, 1)
-        quant_v(1, 2)
-        finish_y("scalar", 1, 0, 0)
-        pack_h("vector", 1, 1)
-        finish_y("scalar", 1, 0, 1)
+        pack_h("scalar", 1, 1)
+        quant_h(1, 0)
+        pack_v("vector", 0, 1)
+        synthesise(0, 0, 0)
         quant_h(0, 1)
-        synthesise(2, 0, 0)
+        synthesise(0, 0, 1)
+        quant_v(0, 1)
+        finish_y("scalar", 0, 0, 0)
         quant_h(1, 1)
-        pack_y("vector", 0, 0)
-        synthesise(2, 0, 1)
+        pack_v("vector", 1, 1)
+        quant_v(1, 1)
         synthesise(0, 1, 0)
-        finish_y("scalar", 2, 0, 0)
-        finish_y("scalar", 2, 0, 1)
-        synthesise(1, 1, 0)
-        synthesise(2, 1, 0)
-        finish_y("scalar", 0, 1, 0)
-        finish_y("scalar", 1, 1, 0)
+        finish_y("scalar", 0, 0, 1)
         synthesise(0, 1, 1)
         synthesise(1, 1, 1)
-        pack_v("vector", 0, 3)
+        synthesise(1, 1, 0)
+        pack_y("vector", 0, 0)
+        finish_y("scalar", 0, 1, 0)
+        finish_y("vector", 0, 1, 1)
         quant_y(0, 0)
+        pack_v("vector", 0, 2)
+        pack_v("scalar", 1, 2)
+        quant_v(1, 2)
+        quant_v(0, 2)
+        synthesise(1, 0, 1)
+        finish_y("scalar", 1, 1, 0)
+        synthesise(1, 0, 0)
+        synthesise(2, 0, 0)
+        finish_y("scalar", 1, 1, 1)
+        synthesise(2, 1, 0)
+        pack_v("vector", 0, 3)
+        finish_y("scalar", 1, 0, 0)
+        finish_y("scalar", 1, 0, 1)
         pack_v("vector", 1, 3)
-        finish_y("scalar", 2, 1, 0)
-        finish_y("scalar", 0, 1, 1)
+        finish_y("scalar", 2, 0, 0)
         quant_v(0, 3)
+        pack_y("vector", 0, 1)
         quant_v(1, 3)
         synthesise(2, 1, 1)
-        synthesise(3, 0, 0)
-        pack_y("vector", 1, 0)
-        synthesise(3, 0, 1)
-        finish_y("scalar", 1, 1, 1)
+        finish_y("scalar", 2, 1, 0)
+        synthesise(2, 0, 1)
         synthesise(3, 1, 0)
         finish_y("scalar", 2, 1, 1)
-        finish_y("scalar", 3, 0, 0)
-        pack_y("vector", 2, 0)
-        finish_y("scalar", 3, 0, 1)
-        quant_y(1, 0)
-        pack_y("vector", 0, 1)
-        synthesise(3, 1, 1)
-        finish_y("scalar", 3, 1, 0)
-        finish_y("scalar", 3, 1, 1)
-        pack_y("vector", 2, 1)
         quant_y(0, 1)
+        synthesise(3, 0, 0)
+        finish_y("scalar", 2, 0, 1)
+        synthesise(3, 0, 1)
+        finish_y("scalar", 3, 1, 0)
+        finish_y("scalar", 3, 0, 0)
+        pack_y("vector", 1, 0)
+        finish_y("scalar", 3, 0, 1)
+        pack_y("vector", 1, 1)
+        quant_y(1, 0)
+        pack_y("vector", 2, 0)
+        quant_y(1, 1)
+        synthesise(3, 1, 1)
+        finish_y("scalar", 3, 1, 1)
+        pack_y("vector", 3, 0)
+        quant_y(2, 0)
+        pack_y("vector", 2, 1)
+        quant_y(3, 0)
         pack_y("scalar", 3, 1)
         quant_y(2, 1)
-        pack_y("vector", 1, 1)
-        quant_y(2, 0)
-        quant_y(1, 1)
-        pack_y("vector", 3, 0)
-        store_scale_rows(nc.sync, 0, 3)
         quant_y(3, 1)
-        quant_y(3, 0)
-        store_scale_rows(nc.scalar, 3, 4)
+        store_scale_rows()

@@ -139,8 +139,8 @@ def tile_damped_basis_estimate_h2_kernel(
         load_b(0, 2)
         load_l(1)
         load_v(1, 0)
-        load_b(1, 0)
         load_v(0, 0)
+        load_b(1, 0)
         load_b(1, 1)
         load_v(0, 1)
         load_b(1, 2)
@@ -195,7 +195,7 @@ def tile_damped_basis_estimate_h2_kernel(
             if engine == "scalar":
                 nc.scalar.copy(out=out, in_=in_)
             elif engine == "gpsimd":
-                nc.gpsimd.tensor_scalar(out=out, in0=in_, scalar1=1.0, scalar2=1.0, op0=ALU.mult, op1=ALU.mult)
+                nc.gpsimd.tensor_scalar(out=out, in0=in_, scalar1=1.0, scalar2=0.0, op0=ALU.mult, op1=ALU.add)
             else:
                 nc.vector.tensor_copy(out=out, in_=in_)
 
@@ -231,7 +231,7 @@ def tile_damped_basis_estimate_h2_kernel(
         def damp(g, h, u):
             if u == 0:
                 h_rows[g, h] = stage.tile([P, PACK, BANK], BF16, name="h_rows", tag="h_rows", bufs=3)
-            for t in (2 * u, 2 * u + 1):
+            for t in (2 * u + 1, 2 * u):
                 c = PACK * g + t
                 nc.vector.scalar_tensor_tensor(
                     out=h_rows[g, h][:, t, :],
@@ -244,12 +244,18 @@ def tile_damped_basis_estimate_h2_kernel(
                 free_banks.append(c_number[g, h, t])
 
         def interleave(engine, rows):
-            packed = stage.tile([P, BANK, PACK], BF16, align_bytes=64, name="packed", tag="packed", bufs=7)
-            copy_on(
-                engine,
-                packed[:].rearrange("p (c i) t -> p c t i", i=4),
-                rows.rearrange("p t (c i) -> p c t i", i=4),
-            )
+            if engine == "gpsimd":
+                packed = stage.tile([P, BANK, PACK], BF16, align_bytes=64, name="packed_g", tag="packed_g", bufs=2)
+            else:
+                packed = stage.tile([P, BANK, PACK], BF16, align_bytes=64, name="packed", tag="packed", bufs=6)
+            if engine == "gpsimd":
+                copy_on(engine, packed[:], rows.rearrange("p t n -> p n t"))
+            else:
+                copy_on(
+                    engine,
+                    packed[:].rearrange("p (c i) t -> p c t i", i=4),
+                    rows.rearrange("p t (c i) -> p c t i", i=4),
+                )
             return packed
 
         def quantise(codes, plane, packed):
@@ -264,7 +270,7 @@ def tile_damped_basis_estimate_h2_kernel(
             quantise(h_codes[g, h][:], h_plane[g, h][:], h_packed[g, h])
 
         def pack_v(engine, g, x):
-            packed = stage.tile([P, BANK, PACK], BF16, align_bytes=64, name="packed", tag="packed", bufs=7)
+            packed = stage.tile([P, BANK, PACK], BF16, align_bytes=64, name="packed", tag="packed", bufs=6)
             copy_on(
                 engine,
                 packed[:].rearrange("p (s m) t -> p m t s", s=PACK),
@@ -297,7 +303,7 @@ def tile_damped_basis_estimate_h2_kernel(
             cols = slice(BANK * h, BANK * (h + 1))
             whole = (x, 1 - h, u) in y_done
             y_done.add((x, h, u))
-            for s in (2 * u, 2 * u + 1):
+            for s in (2 * u + 1, 2 * u):
                 if engine == "scalar":
                     nc.scalar.activation(
                         out=y_rows[x][:, s, cols],
@@ -344,99 +350,99 @@ def tile_damped_basis_estimate_h2_kernel(
                     in_=y_plane[32 * q : 32 * q + 16, :].bitcast(I32),
                 )
 
-        gates(0, 0)
         order_l(0)
+        gates(0, 0)
         nc.vector.tensor_copy(out=affine[:], in_=vec_cols[:, :, 0 : 2 * GROUPS].rearrange("p t a -> p a t"))
         analyse(0, 0, 0)
         order_l(1)
+        analyse(0, 0, 1)
         gates(1, 0)
         damp(0, 0, 0)
-        analyse(0, 0, 1)
         gates(0, 1)
         analyse(1, 0, 0)
+        analyse(1, 0, 1)
         pack_v("scalar", 0, 0)
         pack_v("vector", 1, 0)
-        analyse(1, 0, 1)
-        damp(0, 0, 1)
-        damp(1, 0, 0)
-        analyse(0, 1, 0)
         quant_v(1, 0)
+        damp(0, 0, 1)
+        pack_h("gpsimd", 0, 0)
+        analyse(0, 1, 0)
+        damp(1, 0, 0)
         damp(1, 0, 1)
+        pack_h("gpsimd", 1, 0)
         analyse(0, 1, 1)
-        analyse(1, 1, 0)
-        pack_h("vector", 0, 0)
         damp(0, 1, 0)
-        damp(0, 1, 1)
-        quant_h(0, 0)
         gates(1, 1)
-        pack_h("scalar", 1, 0)
+        damp(0, 1, 1)
         quant_v(0, 0)
-        pack_h("scalar", 0, 1)
-        analyse(1, 1, 1)
-        damp(1, 1, 0)
-        damp(1, 1, 1)
-        pack_h("scalar", 1, 1)
         quant_h(1, 0)
-        pack_v("vector", 0, 1)
+        quant_h(0, 0)
+        pack_h("gpsimd", 0, 1)
+        analyse(1, 1, 0)
+        pack_v("scalar", 0, 1)
+        analyse(1, 1, 1)
+        pack_v("scalar", 1, 1)
         synthesise(0, 0, 0)
-        quant_h(0, 1)
-        synthesise(0, 0, 1)
-        quant_v(0, 1)
         finish_y("scalar", 0, 0, 0)
-        quant_h(1, 1)
-        pack_v("vector", 1, 1)
-        quant_v(1, 1)
-        synthesise(0, 1, 0)
+        synthesise(0, 0, 1)
+        damp(1, 1, 0)
         finish_y("scalar", 0, 0, 1)
-        synthesise(0, 1, 1)
-        synthesise(1, 1, 1)
-        synthesise(1, 1, 0)
-        pack_y("vector", 0, 0)
-        finish_y("scalar", 0, 1, 0)
-        finish_y("vector", 0, 1, 1)
-        quant_y(0, 0)
-        pack_v("vector", 0, 2)
+        damp(1, 1, 1)
+        pack_h("vector", 1, 1)
+        quant_h(0, 1)
+        quant_h(1, 1)
         pack_v("scalar", 1, 2)
-        quant_v(1, 2)
-        quant_v(0, 2)
-        synthesise(1, 0, 1)
-        finish_y("scalar", 1, 1, 0)
+        synthesise(0, 1, 0)
+        quant_v(1, 1)
+        quant_v(0, 1)
+        finish_y("vector", 0, 1, 0)
+        synthesise(0, 1, 1)
         synthesise(1, 0, 0)
-        synthesise(2, 0, 0)
-        finish_y("scalar", 1, 1, 1)
-        synthesise(2, 1, 0)
-        pack_v("vector", 0, 3)
-        finish_y("scalar", 1, 0, 0)
-        finish_y("scalar", 1, 0, 1)
+        pack_v("vector", 0, 2)
+        synthesise(1, 0, 1)
+        finish_y("scalar", 0, 1, 1)
+        quant_v(1, 2)
         pack_v("vector", 1, 3)
-        finish_y("scalar", 2, 0, 0)
-        quant_v(0, 3)
+        finish_y("scalar", 1, 0, 0)
+        synthesise(1, 1, 0)
+        finish_y("scalar", 1, 0, 1)
+        quant_v(0, 2)
+        synthesise(1, 1, 1)
+        synthesise(2, 1, 0)
+        finish_y("scalar", 1, 1, 0)
+        pack_v("vector", 0, 3)
         pack_y("vector", 0, 1)
-        quant_v(1, 3)
-        synthesise(2, 1, 1)
+        quant_v(0, 3)
+        finish_y("scalar", 1, 1, 1)
+        synthesise(2, 0, 0)
         finish_y("scalar", 2, 1, 0)
         synthesise(2, 0, 1)
-        synthesise(3, 1, 0)
-        finish_y("scalar", 2, 1, 1)
-        quant_y(0, 1)
-        synthesise(3, 0, 0)
+        quant_v(1, 3)
+        finish_y("scalar", 2, 0, 0)
+        synthesise(2, 1, 1)
         finish_y("scalar", 2, 0, 1)
-        synthesise(3, 0, 1)
+        quant_y(0, 1)
+        finish_y("scalar", 2, 1, 1)
+        synthesise(3, 1, 0)
+        pack_y("vector", 0, 0)
         finish_y("scalar", 3, 1, 0)
-        finish_y("scalar", 3, 0, 0)
+        synthesise(3, 0, 0)
         pack_y("vector", 1, 0)
-        finish_y("scalar", 3, 0, 1)
-        pack_y("vector", 1, 1)
+        quant_y(0, 0)
         quant_y(1, 0)
-        pack_y("vector", 2, 0)
-        quant_y(1, 1)
         synthesise(3, 1, 1)
+        pack_y("vector", 2, 0)
+        synthesise(3, 0, 1)
+        pack_y("vector", 1, 1)
+        finish_y("scalar", 3, 0, 0)
+        finish_y("scalar", 3, 0, 1)
         finish_y("scalar", 3, 1, 1)
-        pack_y("vector", 3, 0)
         quant_y(2, 0)
+        pack_y("vector", 3, 0)
+        quant_y(1, 1)
         pack_y("vector", 2, 1)
         quant_y(3, 0)
-        pack_y("scalar", 3, 1)
         quant_y(2, 1)
+        pack_y("scalar", 3, 1)
         quant_y(3, 1)
         store_scale_rows()

from contextlib import ExitStack

import concourse.mybir as mybir
from concourse.masks import make_identity

M, K, R, N = 1024, 1536, 1024, 2048
FLOPS = 2 * K * R * M + 2 * R * N * M

F32 = mybir.dt.float32
BF16 = mybir.dt.bfloat16
I32 = mybir.dt.int32
U32 = mybir.dt.uint32
U8 = mybir.dt.uint8
FP8X4 = mybir.dt.float8_e4m3fn_x4
FP4X4 = mybir.dt.float4_e2m1fn_x4
ACT = mybir.ActivationFunctionType
ALU = mybir.AluOpType
AXIS = mybir.AxisListType

P = 128
PACK = 4
BANK = 512
K_PASSES = K // 512
R_PASSES = R // 512
HALVES = M // BANK
GROUPS = N // 512
SPLIT_Y = (0, 1,)
SPLIT_WORDS = (0, 1, 2, 3,)
V_CHUNKS = {0: (0, 1), 1: (1, 2), 2: (2, 4)}


def tile_damped_basis_estimate_h2_kernel(
    tc, b_words, b_scales, l_words, l_scales, v, sigma, alpha, spread, mean, out_0, out_1, out_2
):
    nc = tc.nc
    with ExitStack() as ctx:
        keep = ctx.enter_context(tc.tile_pool(name="keep", bufs=1))
        stage = ctx.enter_context(tc.tile_pool(name="stage", bufs=3))
        psum = ctx.enter_context(tc.psum_pool(name="psum", bufs=1))
        ctx.enter_context(tc.manual_schedule())

        free_banks = [1, 2, 3, 4, 5, 0]

        def bank(number):
            return psum.tile([P, BANK], F32, name="bank%d" % number, tag="bank%d" % number)

        l_raw, l_codes, ls_plane = {}, {}, {}
        for g in range(R_PASSES):
            l_raw[g] = keep.tile([P, K_PASSES, 1024], U8, align_bytes=64, name="l_raw%d" % g)
            l_codes[g] = keep.tile([P, K_PASSES, 1024], U8, align_bytes=64, name="l_codes%d" % g)
            ls_plane[g] = keep.tile([P, K_PASSES, 512], U8, align_bytes=64, name="ls_plane%d" % g)
        ls_raw = keep.tile([P, K_PASSES, R], U8, align_bytes=64)
        bs_plane = keep.tile([P, K_PASSES, M], U8, align_bytes=64)
        b_codes = {}
        for h in range(HALVES):
            for k in range(K_PASSES):
                b_codes[h, k] = keep.tile([P, BANK], U32, align_bytes=64, name="b_codes%d%d" % (h, k))
        v_raw = {}
        for g in range(R_PASSES):
            for lo, hi in V_CHUNKS.values():
                v_raw[g, lo] = keep.tile([P, PACK, 512 * (hi - lo)], BF16, align_bytes=64, name="v_raw%d%d" % (g, lo))
        v_codes, v_plane = {}, {}
        for g in range(R_PASSES):
            for x in range(GROUPS):
                v_codes[g, x] = keep.tile([P, 512], U32, align_bytes=64, name="v_codes%d%d" % (g, x))
                v_plane[g, x] = keep.tile([P, 512], U8, align_bytes=64, name="v_plane%d%d" % (g, x))
        h_codes, h_plane = {}, {}
        for g in range(R_PASSES):
            for h in range(HALVES):
                h_codes[g, h] = keep.tile([P, BANK], U32, align_bytes=64, name="h_codes%d%d" % (g, h))
                h_plane[g, h] = keep.tile([P, BANK], U8, align_bytes=64, name="h_plane%d%d" % (g, h))
        y_plane = keep.tile([P, M], U8, align_bytes=64)
        ident = keep.tile([P, P], F32)
        sigma_block = keep.tile([P, 8, 8], BF16)
        vec_rows = keep.tile([P, 512], BF16)
        ident_bf = keep.tile([P, P], BF16)
        affine = keep.tile([P, 2 * GROUPS, PACK], F32)
        own = keep.tile([P, 8], F32)
        picked = keep.tile([P, 8, 8], F32)
        sigma_col = keep.tile([P, 8], F32)
        sigma_sq = keep.tile([P, 8], F32)
        inv_sigma = keep.tile([P, 8], F32)
        ln_sigma_sq = keep.tile([P, 8], F32)
        ln_alpha = keep.tile([P, HALVES * PACK], F32)
        one = keep.tile([P, 1], F32)
        warm = keep.tile([P, 1], F32)

        v_rows = v.rearrange("(g b t i) n -> g t b i n", g=R_PASSES, t=PACK, i=8)

        def load_v(g, chunk):
            lo, hi = V_CHUNKS[chunk]
            for t in range(PACK):
                nc.sync.dma_start(out=v_raw[g, lo][:, t, :], in_=v_rows[g, t][:, :, 512 * lo : 512 * hi])

        def load_l(g):
            words = l_words.rearrange("k p n -> p k n")[:, :, 1024 * g : 1024 * (g + 1)]
            nc.sync.dma_start(out=l_raw[g][:].bitcast(I32), in_=words.bitcast(I32))

        def load_sigma():
            for g in range(R_PASSES):
                blocks = sigma[512 * g : 512 * (g + 1)].rearrange("(b w) -> b w", w=32)
                nc.sync.dma_start(
                    out=sigma_block[:, PACK * g : PACK * (g + 1), :].rearrange("p c i -> p (c i)"),
                    in_=blocks.unsqueeze(1).to_broadcast([16, 8, 32]),
                )

        def load_rows(first, vector):
            rows = vector.rearrange("(a n) -> a n", n=512)
            nc.sync.dma_start(out=vec_rows[first : first + rows.shape[0], :], in_=rows)

        def load_b(h, k):
            words = b_words[k].rearrange("p n t -> p (n t)")[:, PACK * BANK * h : PACK * BANK * (h + 1)]
            nc.sync.dma_start(out=b_codes[h, k][:].bitcast(I32), in_=words.bitcast(I32))

        def load_scale_rows(plane, rows):
            for q in range(4):
                nc.sync.dma_start(
                    out=plane[32 * q : 32 * q + 4, :, :].bitcast(I32),
                    in_=rows[:, 4 * q : 4 * q + 4, :].rearrange("k r n -> r k n").bitcast(I32),
                )

        nc.vector.memset(ls_raw[:].bitcast(I32), 0)
        nc.vector.memset(bs_plane[:].bitcast(I32), 0)
        nc.vector.memset(one[:], 1.0)
        nc.scalar.activation(out=warm[:], in_=one[:], func=ACT.Ln)
        nc.gpsimd.memset(vec_rows[:], 0.0)
        make_identity(nc, ident_bf[:])
        make_identity(nc, ident[:])

        load_b(0, 0)
        load_sigma()
        load_rows(8, alpha)
        load_rows(0, spread)
        load_rows(4, mean)
        load_l(0)
        load_scale_rows(ls_raw, l_scales)
        load_scale_rows(bs_plane, b_scales)
        load_b(0, 1)
        load_b(0, 2)
        load_l(1)
        load_v(1, 0)
        load_v(0, 0)
        load_b(1, 0)
        load_b(1, 1)
        load_v(0, 1)
        load_b(1, 2)
        load_v(1, 1)
        load_v(0, 2)
        load_v(1, 2)

        nc.vector.tensor_reduce(
            out=own[:], in_=ident[:].rearrange("p (b i) -> p i b", i=8), axis=AXIS.X, op=ALU.add
        )
        vec_cols = psum.tile([P, PACK, P], BF16, name="bank0", tag="bank0")
        for t in range(PACK):
            nc.tensor.transpose(vec_cols[:, t, :], vec_rows[:, t : 512 : PACK], ident_bf[:])
        nc.scalar.activation(
            out=ln_alpha[:].rearrange("p (h m) -> p h m", m=PACK),
            in_=vec_cols[:, :, 8:10].rearrange("p m h -> p h m"),
            func=ACT.Ln,
        )
        nc.vector.tensor_tensor(
            out=picked[:], in0=sigma_block[:], in1=own[:].unsqueeze(1).to_broadcast([P, 8, 8]), op=ALU.mult
        )
        nc.vector.tensor_reduce(out=sigma_col[:], in_=picked[:], axis=AXIS.X, op=ALU.add)
        nc.vector.tensor_tensor(out=sigma_sq[:], in0=sigma_col[:], in1=sigma_col[:], op=ALU.mult)
        nc.vector.reciprocal(out=inv_sigma[:], in_=sigma_col[:])
        nc.scalar.activation(out=ln_sigma_sq[:], in_=sigma_sq[:], func=ACT.Ln)

        ln_alpha_row = {}
        for h in range(HALVES):
            ln_alpha_row[h] = bank(6 + h)
            for m in range(PACK):
                col = PACK * h + m
                nc.tensor.transpose(
                    ln_alpha_row[h][:, P * m : P * (m + 1)],
                    ln_alpha[:, col : col + 1].to_broadcast([P, P]),
                    ident[:],
                )

        def order_l(g):
            nc.vector.tensor_copy(
                out=l_codes[g][:].bitcast(I32).rearrange("p k (t b w) -> p t k b w", t=PACK, w=4),
                in_=l_raw[g][:].bitcast(I32).rearrange("p k (b t w) -> p t k b w", t=PACK, w=4),
            )
            nc.vector.tensor_copy(
                out=ls_plane[g][:].bitcast(I32).rearrange("p k (t b w) -> p t k b w", t=PACK, w=2),
                in_=ls_raw[:, :, 512 * g : 512 * (g + 1)].bitcast(I32).rearrange("p k (b t w) -> p t k b w", t=PACK, w=2),
            )

        c_number, z_number, y_codes, y_done = {}, {}, {}, set()
        c_bank, gate, h_rows, h_packed, v_packed, z_bank, y_rows, y_packed = {}, {}, {}, {}, {}, {}, {}, {}

        def copy_on(engine, out, in_):
            if engine == "scalar":
                nc.scalar.copy(out=out, in_=in_)
            elif engine == "gpsimd":
                nc.gpsimd.tensor_scalar(out=out, in0=in_, scalar1=1.0, scalar2=0.0, op0=ALU.mult, op1=ALU.add)
            else:
                nc.vector.tensor_copy(out=out, in_=in_)

        def analyse(g, h, u):
            for t in (2 * u, 2 * u + 1):
                c_number[g, h, t] = free_banks.pop(0)
                c_bank[g, h, t] = bank(c_number[g, h, t])
                for k in range(K_PASSES):
                    nc.tensor.matmul_mx(
                        out=c_bank[g, h, t][:],
                        lhsT=l_codes[g][:, k, 2 * P * t : 2 * P * (t + 1)].bitcast(FP4X4),
                        lhsT_scale=ls_plane[g][:, k, P * t : P * (t + 1)],
                        rhs=b_codes[h, k][:].bitcast(FP8X4),
                        rhs_scale=bs_plane[:, k, BANK * h : BANK * (h + 1)],
                        start=(k == 0),
                        stop=(k == K_PASSES - 1),
                    )

        def gates(g, h):
            for t in range(PACK):
                c = PACK * g + t
                gate[g, h, t] = stage.tile([P, BANK], F32, name="gate", tag="gate", bufs=16)
                nc.scalar.activation(
                    out=gate[g, h, t][:].rearrange("p (k m) -> p k m", m=PACK),
                    in_=ln_alpha_row[h][:].rearrange("p (m k) -> p k m", m=PACK),
                    func=ACT.Sigmoid,
                    scale=-1.0,
                    bias=ln_sigma_sq[:, c : c + 1],
                )
            if (1 - g, h, 0) in gate:
                free_banks.append(6 + h)

        def damp(g, h, u):
            if u == 0:
                h_rows[g, h] = stage.tile([P, PACK, BANK], BF16, name="h_rows", tag="h_rows", bufs=3)
            for t in (2 * u + 1, 2 * u):
                c = PACK * g + t
                nc.vector.scalar_tensor_tensor(
                    out=h_rows[g, h][:, t, :],
                    in0=c_bank[g, h, t][:],
                    scalar=inv_sigma[:, c : c + 1],
                    in1=gate[g, h, t][:],
                    op0=ALU.mult,
                    op1=ALU.mult,
                )
                free_banks.append(c_number[g, h, t])

        def interleave(engine, rows):
            if engine == "gpsimd":
                packed = stage.tile([P, BANK, PACK], BF16, align_bytes=64, name="packed_g", tag="packed_g", bufs=2)
            else:
                packed = stage.tile([P, BANK, PACK], BF16, align_bytes=64, name="packed", tag="packed", bufs=6)
            if engine == "gpsimd":
                copy_on(engine, packed[:], rows.rearrange("p t n -> p n t"))
            else:
                copy_on(
                    engine,
                    packed[:].rearrange("p (c i) t -> p c t i", i=4),
                    rows.rearrange("p t (c i) -> p c t i", i=4),
                )
            return packed

        def quantise(codes, plane, packed):
            nc.vector.quantize_mx(
                out=codes.bitcast(FP8X4), scales=plane, in_=packed[:].rearrange("p n t -> p (n t)")
            )

        def pack_h(engine, g, h):
            h_packed[g, h] = interleave(engine, h_rows[g, h][:])

        def quant_h(g, h):
            quantise(h_codes[g, h][:], h_plane[g, h][:], h_packed[g, h])

        def pack_v(engine, g, x):
            packed = stage.tile([P, BANK, PACK], BF16, align_bytes=64, name="packed", tag="packed", bufs=6)
            copy_on(
                engine,
                packed[:].rearrange("p (s m) t -> p m t s", s=PACK),
                v_raw[g, min(x, 2)][:, :, 512 * max(x - 2, 0) : 512 * (max(x - 2, 0) + 1)].rearrange("p t (m s) -> p m t s", s=PACK),
            )
            v_packed[g, x] = packed

        def quant_v(g, x):
            quantise(v_codes[g, x][:], v_plane[g, x][:], v_packed[g, x])

        def synthesise(x, h, u):
            for s in (2 * u, 2 * u + 1):
                z_number[x, h, s] = free_banks.pop(0)
                z_bank[x, h, s] = bank(z_number[x, h, s])
                for g in range(R_PASSES):
                    nc.tensor.matmul_mx(
                        out=z_bank[x, h, s][:],
                        lhsT=v_codes[g, x][:, P * s : P * (s + 1)].bitcast(FP8X4),
                        lhsT_scale=v_plane[g, x][:, P * s : P * (s + 1)],
                        rhs=h_codes[g, h][:].bitcast(FP8X4),
                        rhs_scale=h_plane[g, h][:],
                        start=(g == 0),
                        stop=(g == R_PASSES - 1),
                    )

        def finish_y(engine, x, h, u):
            if x not in y_rows:
                y_rows[x] = stage.tile([P, PACK, M], F32, name="y_rows", tag="y_rows", bufs=3)
            target = out_0[512 * x : 512 * (x + 1), :].rearrange("(p s) m -> p s m", s=PACK)
            cols = slice(BANK * h, BANK * (h + 1))
            whole = (x, 1 - h, u) in y_done
            y_done.add((x, h, u))
            for s in (2 * u + 1, 2 * u):
                if engine == "scalar":
                    nc.scalar.activation(
                        out=y_rows[x][:, s, cols],
                        in_=z_bank[x, h, s][:],
                        func=ACT.Identity,
                        scale=affine[:, x, s : s + 1],
                        bias=affine[:, GROUPS + x, s : s + 1],
                    )
                else:
                    nc.vector.tensor_scalar(
                        out=y_rows[x][:, s, cols],
                        in0=z_bank[x, h, s][:],
                        scalar1=affine[:, x, s : s + 1],
                        scalar2=affine[:, GROUPS + x, s : s + 1],
                        op0=ALU.mult,
                        op1=ALU.add,
                    )
                free_banks.append(z_number[x, h, s])
                if whole and x not in SPLIT_Y:
                    nc.sync.dma_start(out=target[:, s, :], in_=y_rows[x][:, s, :])
            rows = slice(2 * u, 2 * u + 2)
            if x in SPLIT_Y:
                nc.sync.dma_start(out=target[:, rows, cols], in_=y_rows[x][:, rows, cols])

        def pack_y(engine, x, h):
            y_packed[x, h] = interleave(engine, y_rows[x][:, :, BANK * h : BANK * (h + 1)])

        def quant_y(x, h):
            whole = x in y_codes
            if not whole:
                y_codes[x] = stage.tile([P, M], U32, align_bytes=64, name="y_codes", tag="y_codes", bufs=3)
            cols = slice(BANK * h, BANK * (h + 1))
            quantise(y_codes[x][:, cols], y_plane[4 * x :, cols], y_packed[x, h])
            words = out_1[x].rearrange("p m t -> p (m t)").bitcast(I32)
            if x in SPLIT_WORDS:
                nc.sync.dma_start(out=words[:, cols], in_=y_codes[x][:, cols].bitcast(I32))
            elif whole:
                nc.sync.dma_start(out=words, in_=y_codes[x][:].bitcast(I32))

        def store_scale_rows():
            for q in range(4):
                nc.scalar.dma_start(
                    out=out_2[:, 4 * q : 4 * q + 4, :].bitcast(I32),
                    in_=y_plane[32 * q : 32 * q + 16, :].bitcast(I32),
                )

        order_l(0)
        gates(0, 0)
        nc.vector.tensor_copy(out=affine[:], in_=vec_cols[:, :, 0 : 2 * GROUPS].rearrange("p t a -> p a t"))
        analyse(0, 0, 0)
        order_l(1)
        analyse(0, 0, 1)
        gates(1, 0)
        damp(0, 0, 0)
        gates(0, 1)
        analyse(1, 0, 0)
        analyse(1, 0, 1)
        pack_v("scalar", 0, 0)
        pack_v("vector", 1, 0)
        quant_v(1, 0)
        damp(0, 0, 1)
        pack_h("gpsimd", 0, 0)
        analyse(0, 1, 0)
        damp(1, 0, 0)
        damp(1, 0, 1)
        pack_h("gpsimd", 1, 0)
        analyse(0, 1, 1)
        damp(0, 1, 0)
        gates(1, 1)
        damp(0, 1, 1)
        quant_v(0, 0)
        quant_h(1, 0)
        quant_h(0, 0)
        pack_h("gpsimd", 0, 1)
        analyse(1, 1, 0)
        pack_v("scalar", 0, 1)
        analyse(1, 1, 1)
        pack_v("scalar", 1, 1)
        synthesise(0, 0, 0)
        finish_y("scalar", 0, 0, 0)
        synthesise(0, 0, 1)
        damp(1, 1, 0)
        finish_y("scalar", 0, 0, 1)
        damp(1, 1, 1)
        pack_h("vector", 1, 1)
        quant_h(0, 1)
        quant_h(1, 1)
        pack_v("scalar", 1, 2)
        synthesise(0, 1, 0)
        quant_v(1, 1)
        quant_v(0, 1)
        finish_y("vector", 0, 1, 0)
        synthesise(0, 1, 1)
        synthesise(1, 0, 0)
        pack_v("vector", 0, 2)
        synthesise(1, 0, 1)
        finish_y("scalar", 0, 1, 1)
        quant_v(1, 2)
        pack_v("vector", 1, 3)
        finish_y("scalar", 1, 0, 0)
        synthesise(1, 1, 0)
        finish_y("scalar", 1, 0, 1)
        quant_v(0, 2)
        synthesise(1, 1, 1)
        synthesise(2, 1, 0)
        finish_y("scalar", 1, 1, 0)
        pack_v("vector", 0, 3)
        pack_y("vector", 0, 1)
        quant_v(0, 3)
        finish_y("scalar", 1, 1, 1)
        synthesise(2, 0, 0)
        finish_y("scalar", 2, 1, 0)
        synthesise(2, 0, 1)
        quant_v(1, 3)
        finish_y("scalar", 2, 0, 0)
        synthesise(2, 1, 1)
        finish_y("scalar", 2, 0, 1)
        quant_y(0, 1)
        finish_y("scalar", 2, 1, 1)
        synthesise(3, 1, 0)
        pack_y("vector", 0, 0)
        finish_y("scalar", 3, 1, 0)
        synthesise(3, 0, 0)
        pack_y("vector", 1, 0)
        quant_y(0, 0)
        quant_y(1, 0)
        synthesise(3, 1, 1)
        pack_y("vector", 2, 0)
        synthesise(3, 0, 1)
        pack_y("vector", 1, 1)
        finish_y("scalar", 3, 0, 0)
        finish_y("scalar", 3, 0, 1)
        finish_y("scalar", 3, 1, 1)
        quant_y(2, 0)
        pack_y("vector", 3, 0)
        quant_y(1, 1)
        pack_y("vector", 2, 1)
        quant_y(3, 0)
        quant_y(2, 1)
        pack_y("scalar", 3, 1)
        quant_y(3, 1)
        store_scale_rows()
